import numpy as np, ml_dtypes
CORES = [21,85,149,213,277,341,405,469]
N = 8
F = 128
def setup_inputs(rng):
    return {"ah": rng.standard_normal((N, 128, 128), dtype=np.float32).astype(ml_dtypes.bfloat16), "al": (rng.standard_normal((N, 128, 128), dtype=np.float32) / 256).astype(ml_dtypes.bfloat16), "bh": rng.standard_normal((N, 128, F), dtype=np.float32).astype(ml_dtypes.bfloat16), "bl": (rng.standard_normal((N, 128, F), dtype=np.float32) / 256).astype(ml_dtypes.bfloat16)}
def setup_inputs_big(rng):
    d = setup_inputs(rng)
    for k in ("ah", "al", "bh", "bl"): d[k] = (d[k].astype(np.float32) * 1024.0).astype(d[k].dtype)
    return d
def setup_inputs_small(rng):
    d = setup_inputs(rng)
    for k in ("ah", "al", "bh", "bl"): d[k] = (d[k].astype(np.float32) * (1 / 1024.0)).astype(d[k].dtype)
    return d
def setup_inputs_apart(rng):
    d = setup_inputs(rng)
    f = (10.0 ** rng.permutation(np.linspace(-1.5, 1.5, N))).astype(np.float32).reshape(N, 1, 1)
    for k in ("ah", "al", "bh", "bl"): d[k] = (d[k].astype(np.float32) * f).astype(d[k].dtype)
    return d
def reference(ah, al, bh, bl):
    AH, AL, BH, BL = ah.astype(np.float64), al.astype(np.float64), bh.astype(np.float64), bl.astype(np.float64)
    s = sum((AH[j] + AL[j]).T @ (BH[j] + BL[j]) for j in range(N))
    s = s.astype(np.float32 if ah.dtype != np.float64 else np.float64)
    return {"y": np.broadcast_to(s, (N,) + s.shape)}

from concourse.bass import DstId, RemoteDMATransfer
from concourse.mybir import AluOpType

F = 128

SCRATCH = {
    "ah_s": ("sbuf", [128, 128], "bfloat16"),
    "al_s": ("sbuf", [128, 128], "bfloat16"),
    "bh_s": ("sbuf", [128, F], "bfloat16"),
    "bl_s": ("sbuf", [128, F], "bfloat16"),
    "acc0": ("psum", [128, F], "float32"),
    "acc1": ("psum", [128, F], "float32"),
    "acc2": ("psum", [128, F], "float32"),
    "acc3": ("psum", [128, F], "float32"),
    "mine": ("sbuf", [128, F], "float32"),
    "peer": ("sbuf", [128, 3 * F], "float32"),
    "far": ("sbuf", [128, F], "float32"),
    "out": ("sbuf", [128, F], "float32"),
}
SEMAPHORES = ["ldh", "ldl", "mm", "cp", "arr1", "arr2", "sent", "va", "fin", "st"]


def _engines(mask):
    return bin(mask).count("1")


def _plane_peers(c, T, topo):
    return [d for d in T.cores if d != c and topo.same_plane(c, d)]


def _cable_peer(c, T, topo):
    return [d for d in T.cores
            if topo.rack(topo.host(d)) != topo.rack(topo.host(c)) and topo.may_write(c, d)
            and topo.chip(d) == topo.chip(c)][0]


def rank_program(g, core, T, topo):
    if T.rank_of(core) is None:
        return
    S = T.sem
    add = AluOpType.add
    peers = _plane_peers(core, T, topo)
    far = _cable_peer(core, T, topo)

    g.sync.dma_start(T.ah_s[:], T.ah[:]).then_inc(S.ldh, 16)
    g.scalar.dma_start(T.bh_s[:], T.bh[:]).then_inc(S.ldh, 16)
    g.sync.dma_start(T.al_s[:], T.al[:]).then_inc(S.ldl, 16)
    g.scalar.dma_start(T.bl_s[:], T.bl[:]).then_inc(S.ldl, 16)

    te = g.tensor
    te.wait_ge(S.ldh, 32)
    te.matmul(T.acc0[:], T.ah_s[:], T.bh_s[:], start=True, stop=False).then_inc(S.mm, 1)
    te.wait_ge(S.ldl, 32)
    te.matmul(T.acc0[:], T.al_s[:], T.bh_s[:], start=False, stop=False).then_inc(S.mm, 1)
    te.matmul(T.acc0[:], T.ah_s[:], T.bl_s[:], start=False, stop=False).then_inc(S.mm, 1)
    te.matmul(T.acc0[:], T.al_s[:], T.bl_s[:], start=False, stop=True).then_inc(S.mm, 1)

    v = g.vector
    v.wait_ge(S.mm, 4)
    v.tensor_copy(T.mine[:], T.acc0[:]).then_inc(S.cp, 1)

    m1 = topo.mask(core, peers[0])
    for d in peers:
        m1 &= topo.mask(core, d)
    k = [c for c in T.cores if c == core or c in peers].index(core)
    order = peers[k:] + peers[:k]
    ids, dsts = [], []
    for d in order:
        rid, pid = topo.addr(d, core)
        slot = _plane_peers(d, T, topo).index(core)
        ids.append(DstId(rid=rid, pnc=pid))
        dsts.append(T.peer[:, slot * F:(slot + 1) * F])
    g.wait_ge(S.cp, 1)
    g.remote_dma_fused([RemoteDMATransfer(dst_ids=ids, dma_engine_mask=m1, remote_sem=S.arr1,
                                          srcs=[T.mine[:]], dsts=dsts, alu_op=0)], local_sem=S.sent)

    got1 = sum(_engines(topo.mask(d, core)) for d in peers)
    m2 = topo.mask(core, far)
    rid, pid = topo.addr(far, core)
    g.wait_ge(S.arr1, got1)
    g.remote_dma_fused([RemoteDMATransfer(dst_ids=[DstId(rid=rid, pnc=pid)], dma_engine_mask=m2, remote_sem=S.arr2,
                                          srcs=[T.mine[:]] + [T.peer[:, s * F:(s + 1) * F] for s in range(3)],
                                          dsts=[T.far[:]], alu_op=1)], local_sem=S.sent)

    v.wait_ge(S.arr1, got1)
    v.tensor_tensor(T.acc1[:], T.acc0[:], T.peer[:, 0:F], add).then_inc(S.va, 1)
    v.wait_ge(S.va, 1)
    v.tensor_tensor(T.acc2[:], T.acc1[:], T.peer[:, F:2 * F], add).then_inc(S.va, 1)
    v.wait_ge(S.va, 2)
    v.tensor_tensor(T.acc3[:], T.acc2[:], T.peer[:, 2 * F:3 * F], add).then_inc(S.va, 1)
    v.wait_ge(S.va, 3)

    v.wait_ge(S.arr2, _engines(topo.mask(far, core)))
    v.tensor_tensor(T.out[:], T.acc3[:], T.far[:], add).then_inc(S.fin, 1)
    g.sync.wait_ge(S.fin, 1)
    g.sync.dma_start(T.y[:], T.out[:]).then_inc(S.st, 16)
    g.sync.wait_ge(S.st, 16)

    g.wait_ge(S.sent, _engines(m1) + _engines(m2))
